import numpy as np, ml_dtypes
CORES = [3,11,19,27,35,43]
N = 6
BF = ml_dtypes.bfloat16
NN, P, LN, RO = 512, 1, 512, 4
W = 8 * NN
ACT = (P * np.arange(LN)[None, :] + np.arange(RO)[:, None] % P).reshape(-1)
def states(rng):
    return (0.125 + 1.375 * rng.random((N, 8, 16, W))) * rng.choice(np.array([0.75, 1.0, 1.25]), (N, 8, 16, 1))
def parts(rng, few=(4, 6, 10, 16, 32)):
    o = rng.permutation(NN).reshape(NN // 32, 32); cl = np.empty(NN, np.int64); cl[o.reshape(-1)] = np.arange(NN) // 32
    sz = rng.permutation(np.resize(np.array(few), NN // 32))[cl]
    def member(c, n, shape, stray):
        m = o[c, (rng.random(shape) * n).astype(np.int64)]
        return np.where(rng.random(shape) < stray, rng.integers(0, NN, shape), m)
    ka = member(cl, sz, (N, 8, 16, NN), 0.04)
    for c in range(5):
        e = member(cl, sz, (N, 8, NN), 0.0); np.put_along_axis(ka, (e & 3)[:, :, None], e[:, :, None], 2)
    nm = 8 * member(cl, 32, (N, 8, 8, NN), 0.2) + rng.integers(0, 8, (N, 8, 8, NN))
    own = np.take_along_axis(ka, rng.integers(0, 4, (N, 8, 1, NN)), 2)[:, :, 0]
    wide_ = np.where(rng.random((N, 8, NN)) < 0.2, 32, sz)
    pv = np.where(rng.random((N, 8, NN)) < 0.35, own, member(cl, wide_, (N, 8, NN), 0.03))
    own = np.take_along_axis(ka[..., ACT], rng.integers(0, 4, (N, 8, 1, RO * LN)), 2)[:, :, 0]
    sp = np.where(rng.random((N, 8, RO * LN)) < 0.6, own, member(cl[ACT], 32, (N, 8, RO * LN), 0.1))
    proto = rng.integers(0, 4, (N, 8, 16, NN // 32))[..., cl]
    xa = np.where(rng.random((N, 8, 16, NN)) < 0.3, proto, rng.integers(0, 4, (N, 8, 16, NN)))
    return ka, nm, xa, pv, sp
def pack(ka, nm, xa, s, pv, sp):
    return {"ka": np.ascontiguousarray(ka).reshape(N, 128, NN).astype(np.int32), "nm": np.ascontiguousarray(nm).reshape(N, 64, NN).astype(np.int32),
            "xa": np.ascontiguousarray(xa).reshape(N, 128, NN).astype(np.float32).astype(BF), "s0": np.ascontiguousarray(s).reshape(N, 128, W).astype(np.float32).astype(BF),
            "pv": np.ascontiguousarray(pv).astype(np.int32), "sp": np.ascontiguousarray(sp).astype(np.int32)}
def setup_inputs(rng):
    ka, nm, xa, pv, sp = parts(rng)
    return pack(ka, nm, xa, states(rng), pv, sp)
def setup_inputs_spread(rng):
    ka, nm, xa, pv, sp = parts(rng)
    s = (0.125 + 0.875 * rng.random((N, 8, 16, W))) * np.exp2(rng.integers(-1, 2, (N, 8, 1, W)))
    s = np.where(rng.random((N, 8, 1, W)) > 0.0625, s, 0.0625)
    return pack(ka, nm, xa, s, pv, sp)
def setup_inputs_ends(rng):
    ka, nm, xa, pv, sp = parts(rng)
    def ends(x, hi, share):
        return np.where(rng.random(x.shape) < share, hi * rng.integers(0, 2, x.shape), x)
    kind = rng.integers(0, 4, (N, 8, 1, NN))
    ka = np.where(kind == 0, 0, np.where(kind == 1, NN - 1, ends(ka, NN - 1, 0.7)))
    nm = ends(nm, W - 1, 0.8); pv = ends(pv, NN - 1, 0.75); sp = ends(sp, NN - 1, 0.75)
    kind = rng.integers(0, 4, (N, 8, 1, NN))
    xa = np.where(kind == 0, 0, np.where(kind == 1, 3, 3 * rng.integers(0, 2, (N, 8, 16, NN))))
    u = P * (LN - 1); v = 0 if u == NN - 1 else NN - 1
    ka[:, :, :15, u] = 0; ka[:, :, 15, u] = NN - 1
    ka[:, :, 1:7, v] = 0; ka[:, :, 8:15, v] = rng.integers(0, NN - 3, (N, 8, 7)); ka[:, :, 15, v] = NN - 1
    ka[:, 0::2, 0, v] = 2; ka[:, 0::2, 7, v] = NN - 3; ka[:, 1::2, 0, v] = NN - 3; ka[:, 1::2, 7, v] = 2
    nm[:, :, 7, v] = W - 1; pv[:, :, u] = v
    for z in (2, NN - 3):
        xa[0::2, :, :, z] = xa[0::2, :, :, u]; xa[1::2, :, :, z] = 3 - xa[1::2, :, :, u]
    u2 = P * (LN - 2); v2 = 1
    ka[:, :, :, u2] = 5; ka[:, :, :7, v2] = 5; ka[:, :, 7, v2] = 0; ka[:, :, 8:, v2] = 5
    pv[:, :, u2] = v2; sp[:, :, LN - 2] = 7; xa[1::2, :, :, 0] = 3 - xa[1::2, :, :, u2]
    s = np.where(rng.random((N, 8, 16, W)) < 0.65, 2.0 - 1.9375 * rng.integers(0, 2, (N, 8, 16, W)), states(rng))
    s[..., W - 2] = 2.0625 - s[..., W - 1]
    return pack(ka, nm, xa, s, pv, sp)
def setup_inputs_corners(rng):
    ka, nm, xa, pv, sp = parts(rng); u = np.arange(NN); h = NN // 2
    for q in range(N):
        for g in range(8):
            c = (g + q) % 8
            if c == 0: pv[q, g] = u; sp[q, g] = ACT
            if c == 1: ka[q, g] = rng.integers(0, NN, NN)[None, :]
            if c == 2:
                ka[q, g] = 2 * rng.integers(0, h, (16, NN)) + (u >= h)[None, :]
                pv[q, g] = np.where(u < h, h + rng.integers(0, h, NN), rng.integers(0, h, NN))
            if c == 3:
                ka[q, g, :15] = rng.integers(0, h, (15, NN)); ka[q, g, 15] = NN - 1; nm[q, g, 7] = 8 * rng.permutation(NN) + 7
            if c == 4: xa[q, g] = 3
            if c == 5:
                ka[q, g, :7] = np.arange(7)[:, None]; ka[q, g, 8:15] = np.arange(7)[:, None]; ka[q, g, 15] = 0; ka[q, g, 7] = rng.integers(7, NN, NN)
            if c == 6: ka[q, g] = rng.permutation(NN)[:16][np.argsort(rng.random((16, NN)), axis=0)]
            if c == 7:
                pv[q, g] = NN - 1 if rng.random() < 0.5 else int(rng.integers(0, NN)); sp[q, g] = int(rng.integers(1, NN))
                k = rng.integers(0, 3, NN)[None, :]
                off = np.where(k == 0, 0, np.where(k == 1, (np.arange(16) == 15)[:, None].astype(np.int64), 1))
                xa[q, g] = (rng.integers(0, 4, (16, 1)) + off) & 3
    return pack(ka, nm, xa, states(rng), pv, sp)
def setup_inputs_ties(rng):
    ka, nm, xa, pv, sp = parts(rng, (4, 8, 16, 32))
    row = rng.integers(0, 16, (N, 8, 1, 1)); flip = rng.integers(0, 2, (N, 8, 1, NN))
    xa = (rng.integers(0, 4, (N, 8, 16, 1)) + (np.arange(16)[:, None] == row) * flip) & 3
    ka[:, :, 8:, ::2] = ka[:, :, :8, ::2]; ka[:, :, 5:8, 1::2] = ka[:, :, 3:4, 1::2]
    return pack(ka, nm, xa, states(rng), pv, sp)
def check_ranges(d):
    bad = []
    for k, lo, hi in (("ka", 0, NN - 1), ("nm", 0, W - 1), ("xa", 0, 3), ("pv", 0, NN - 1), ("sp", 0, NN - 1)):
        v = np.asarray(d[k]).astype(np.float64)
        if not (np.min(v) >= lo and np.max(v) <= hi and np.all(v == np.floor(v))): bad.append("range of " + k)
    v = np.asarray(d["s0"]).astype(np.float64)
    if not (np.min(v) >= 0.0625 and np.max(v) <= 2): bad.append("range of s0")
    return bad
def reference(ka, nm, xa, s0, pv, sp):
    a = ka.astype(np.int64).reshape(N, 8, 16, NN); x = xa.astype(np.float32).reshape(N, 8, 16, NN); S = s0.astype(np.float64).reshape(N, 8, 16, W)
    own = np.broadcast_to(8 * np.arange(NN)[None, :] + np.arange(8)[:, None], (N, 8, 8, NN))
    nam = np.concatenate([own, nm.astype(np.int64).reshape(N, 8, 8, NN)], axis=2)
    p = pv.astype(np.int64).reshape(N, 8, NN); spare = sp.astype(np.int64).reshape(N, 8, RO * LN); out = np.zeros((N, 8, 16, RO * LN))
    for t in range(RO):
        u = P * np.arange(LN) + t % P; v = p[:, :, u]
        au = a[:, :, :, u]; su = nam[:, :, :, u]
        av = np.take_along_axis(a, v[:, :, None], 3); nv = np.take_along_axis(nam, v[:, :, None], 3)
        eq = au[:, :, :, None, :] == av[:, :, None, :, :]
        m = np.where(np.any(eq, axis=3), np.take_along_axis(nv, np.argmax(eq, axis=3), 2), su)
        left = np.take_along_axis(S, su.reshape(N, 8, 1, 16 * LN), 3); right = np.take_along_axis(S, m.reshape(N, 8, 1, 16 * LN), 3)
        gate = 0.5 + 0.5 * np.tanh(0.5 * left)
        O = np.sum((gate * right).reshape(N, 8, 16, 16, LN), axis=3)
        out[:, :, :, t * LN:(t + 1) * LN] = O
        c = av[:, :, :8]; ok = (c != u) & ~np.any(eq, axis=2)[:, :, :8]
        xw = np.take_along_axis(x, c.reshape(N, 8, 1, 8 * LN), 3).reshape(N, 8, 16, 8, LN)
        cnt = np.sum(xw == x[:, :, :, u][:, :, :, None, :], axis=2)
        j = np.argmax(np.where(ok, cnt, -1), axis=2); some = np.any(ok, axis=2)
        w = np.where(some, np.take_along_axis(c, j[:, :, None], 2)[:, :, 0], spare[:, :, t * LN:(t + 1) * LN])
        p[:, :, u] = w
        if t == RO - 1: break
        row = v & 3; place = 8 * u + row
        same = np.take_along_axis(au, row[:, :, None], 2) == v[:, :, None]
        new = np.tanh(0.125 * O + np.where(same, np.take_along_axis(S, place[:, :, None], 3), 0.0))
        sh = 1 + t % (N - 1)
        gv = np.roll(np.roll(v, sh, axis=0), 1, axis=1); gnew = np.roll(np.roll(new, sh, axis=0), 1, axis=1); grow = 4 + (gv & 3)
        np.put_along_axis(S, place[:, :, None], new, 3); np.put_along_axis(S, (8 * u + grow)[:, :, None], gnew, 3)
        rr = 8 + (w & 7); an = np.array(au); nn = np.array(su)
        np.put_along_axis(an, row[:, :, None], v[:, :, None], 2); np.put_along_axis(an, grow[:, :, None], gv[:, :, None], 2)
        np.put_along_axis(an, rr[:, :, None], np.where(some[:, :, None], w[:, :, None], np.take_along_axis(au, rr[:, :, None], 2)), 2)
        np.put_along_axis(nn, rr[:, :, None], np.where(some[:, :, None], (8 * v + j)[:, :, None], np.take_along_axis(su, rr[:, :, None], 2)), 2)
        a[:, :, :, u] = an; nam[:, :, :, u] = nn
    return {"yo": out.reshape(N, 128, RO * LN).astype(np.float32), "yp": p.astype(np.float32)}

def check_inputs(d):
    bad = list(check_ranges(d))
    if not bad:
        for name, y in reference(**d).items():
            for q in range(N):
                v = np.abs(np.asarray(y[q], np.float64)); s = np.sqrt(np.mean(v * v))
                if v.max() > 4 * s or s < 2.0 ** 1: bad.append('%s of rank %d is uneven or too small' % (name, q))
    return bad

from concourse.bass import DstId, RemoteDMATransfer
from concourse.mybir import dt, AluOpType, AxisListType, ActivationFunctionType

AL = AluOpType
AF = ActivationFunctionType
NR, RO = 6, 4
CHS = [[0, 80, 160, 224, 256]] * 3 + [[0, 64, 128, 192, 232, 256]]
REDS = [["dma", "dma", "dma", "scan"]] * 3 + [["pe", "scan", "pe", "scan", "scan"]]
SENDS = [[0, 1], [2], [3]]
MODE = ["vvvaaaaaaaaaaaaa"] * 4
YVS = [0, 16, 16, 128]
COSTS = [(0.42, 1.56, 3.8), (0.42, 1.1, 2.0), (0.6, 2.0, 5.5)]
YB = 4104
NMPE = False
XRV = 2
TRIES = 3000
SEEDS = None

INC = False
ZPE = False
TK16 = True
F32, BF, I32, U16, F16 = "float32", "bfloat16", "int32", "uint16", "float16"
SB = {
    "X": (8200, F32), "G": (8192, F32), "P1": (4096, F32), "P2": (4096, F32), "AD": (8192, BF), "SCN": (8192, BF),
    "EX": (4096, BF), "XR": (4096, BF), "OUT": (2048, F32), "SND": (1536, F32),
    "LT": (1536, F32), "GU": (768, BF), "UT": (1280, BF), "TA": (512, F32), "Z8": (512, F32), "H8": (512, F32),
    "KI": (512, I32), "K": (512, BF), "AV": (512, BF), "XA": (512, BF), "INI": (512, I32), "INF": (512, F32),
    "IDX": (2048, U16), "NL": (1024, U16), "CL": (256, U16), "LST": (512, U16), "NMF": (256, F32), "TN": (256, F32),
    "SPT": (256, F32), "TS": (256, F32), "BS": (256, F32), "U": (256, BF), "NQ": (256, BF), "SM": (256, BF),
    "SG": (512, BF), "NF": (512, BF), "TI": (512, F32), "MK": (512, BF), "TK": (512, F16 if TK16 else F32), "YP": (512, F32),
    "D0": (2048, BF), "D1": (256, BF), "D2": (1280, BF),
    "TW": (256, I32), "TF": (256, F32), "UC": (256, BF), "UW": (32, BF), "UV": (32, F32), "ONE": (128, BF),
    "ROW": (160, BF), "F16": (128, BF), "F8": (128, BF), "F4": (128, BF), "PI": (8, I32), "PF": (8, F32),
    "CO": (32, F32), "MD": (128 * 14, BF), "MH": (288, F16), "S8": (8, F32), "MB": (2048, BF), "MM": (128 * 20, BF), "MS": (144 * 12, BF),
    "MF": (128 * 2 + 144 * 3, F32),
}
SCRATCH = {k: ("sbuf", [128, w], d) for k, (w, d) in SB.items()}
for _b in range(8):
    SCRATCH["pb%d" % _b] = ("psum", [128, 512], F32)
SEMAPHORES = ["sv", "sa", "sp_", "sg", "ls"] + ["rt%d" % t for t in range(3)] + ["ru%d" % t for t in range(3)] + \
             ["d%d" % i for i in range(40)]
ESEM = {"v": "sv", "a": "sa", "p": "sp_", "g": "sg"}


def A(name, c0=0, c1=None, st=1, p0=0, p1=128, ps=1):
    if c1 is None:
        c1 = 512 if name[:2] == "pb" else SB[name][0]
    return ("ap", name, p0, p1, ps, c0, c1, st)


def IND(win, off):
    return ("ind", win, off)


def HB(name, r0, r1, c0, c1):
    return ("hbm", name, r0, r1, c0, c1)


def ncol(a):
    if a[0] == "ind":
        return 16 * ncol(a[2])
    return len(range(a[5], a[6], a[7]))


def wide(a):
    if a[1][:2] == "pb":
        return 4
    return 2 if SB[a[1]][1] in (BF, U16, F16) else 4


def touch(a):
    if not isinstance(a, tuple) or a[0] == "hbm":
        return []
    if a[0] == "ind":
        return touch(a[1]) + touch(a[2])
    if a[7] == 1:
        m = ((1 << (a[6] - a[5])) - 1) << a[5]
    else:
        m = 0
        for c in range(a[5], a[6], a[7]):
            m |= 1 << c
    if a[1] in ("INI", "INF", "CO"):
        return [(a[1] + str(q), m) for q in range(a[2] // 32, (a[3] + 31) // 32)]
    return [(a[1], m)]


def program(PE_NS, GATH, SCAT):
    ops = []
    nd = [0]
    tag = [0]

    def add(eng, kind, args, outs, ins, dur, lat=0.0, sem=None):
        rd, wr = [], []
        for a in ins:
            rd += touch(a)
        for a in outs:
            if a[0] == "ind":
                wr += touch(a[1]); rd += touch(a[2])
            else:
                wr += touch(a)
        ops.append({"e": eng, "k": kind, "a": args, "r": rd, "w": wr, "d": dur, "l": lat, "s": sem, "x": [], "t": tag[0]})
        return len(ops) - 1

    def cyc(out, ins, full):
        if out[0] == "ind":
            return SCAT * ncol(out)
        if ins[0][0] == "ind":
            return GATH * ncol(out)
        return full * ncol(out)

    def vt(n):
        return 50.0 + 0.83 * max(64.0, n)

    def half(out, *ins):
        return 0.5 if all(a[0] == "ap" and wide(a) == 2 for a in (out,) + ins) else 1.0

    def ts(out, i0, s1, op0, s2=None, op1=None):
        add("v", "ts", (out, i0, s1, s2, op0, op1), [out], [i0, s1, s2], vt(cyc(out, [i0], half(out, i0))))

    def tt(out, i0, i1, op):
        ps = i0[0] == "ap" and (i0[1][:2] == "pb" or i1[1][:2] == "pb")
        add("v", "tt", (out, i0, i1, op), [out], [i0, i1], vt(cyc(out, [i0], 1.0 if ps else 2.0)))

    def cp(out, i0):
        add("v", "cp", (out, i0), [out], [i0], vt(cyc(out, [i0], half(out, i0))))

    def ms(out, val):
        add("v", "ms", (out, val), [out], [], vt(ncol(out) * wide(out) / 4.0))

    def scan(out, d0, d1, init, op0, op1):
        add("v", "scan", (out, d0, d1, init, op0, op1), [out], [d0, d1], vt(ncol(out) * half(out, d0, d1)))

    def vtr(out, i0):
        add("v", "tr", (out, i0), [out], [i0], vt(ncol(out) * half(out, i0)))

    def act(out, i0, f, bias=0.0, scale=1.0):
        add("a", "act", (out, i0, f, bias, scale), [out], [i0, bias, scale], 15.0 + vt(cyc(out, [i0], 1.0)))

    def mm(out, pairs, start=True, stop=True):
        d = 0.0
        ins = []
        for l, r in pairs:
            d += max(64, ncol(r)) * (4 if wide(r) == 4 else 1) * PE_NS + 5.0
            ins += [l, r]
        add("p", "mm", (out, pairs, start, stop), [out], ins, d, 60.0)

    def iota(out, pat, base, mult):
        add("g", "iota", (out, pat, base, mult), [out], [], 130.0 + 1.66 * ncol(out))

    def dma(q, out, i0, nbytes, acc=False):
        s = "d%d" % nd[0]
        nd[0] += 1
        add(q, "dma", (out, i0, acc), [out], [i0] + ([out] if acc else []), 1000.0 if q == "g" else 100.0,
            1800.0 + nbytes * (0.42 if acc else 0.21), s)

    def send(t, out, i0, sem, nbytes):
        return add("g", "send", (t, out, i0, sem), [], [i0], 800.0, 2000.0 + nbytes * 1.3, "ls")

    def recv(out, sem, sends):
        i = add(None, "recv", (len(sends),), [out], [], 0.0, 0.0, sem)
        ops[i]["x"] = list(sends)

    dma("s", A("INI", p0=96, p1=104), HB("pv", 0, 8, 0, 512), 2048)
    dma("s", A("INI", p0=64, p1=96), HB("sp", 0, 8, 0, 2048), 2048)
    dma("s", A("INI", p0=0, p1=64), HB("nm", 0, 64, 0, 512), 2048)
    dma("s", A("KI"), HB("ka", 0, 128, 0, 512), 2048)
    dma("s", A("XA"), HB("xa", 0, 128, 0, 512), 1024)
    iota(A("PI", 0, 2), [[16, 2]], 0, 1)
    dma("g", A("X", 0, 4096), HB("s0", 0, 128, 0, 4096), 16384)
    iota(A("ROW"), [[1, 160]], 0, 0)
    iota(A("F8"), [[1, 16], [0, 8]], 0, 0)
    iota(A("F4"), [[1, 32], [0, 4]], 0, 0)
    iota(A("UC"), [[2, 256]], -256, 0)
    iota(A("UV"), [[16, 32]], -256, 1)

    pi = lambda c: A("PI", c, c + 1)
    ts(pi(2), pi(0), 4, AL.arith_shift_right)
    ts(pi(3), pi(0), 3, AL.arith_shift_right)
    ts(pi(4), pi(0), 7, AL.bitwise_and)
    ts(pi(5), pi(0), 3, AL.bitwise_and)
    ts(pi(6), pi(1), 127, AL.bitwise_and)
    ts(pi(7), pi(6), 3, AL.arith_shift_right)
    cp(A("PF"), A("PI"))
    pf = lambda c, p0=0, p1=128: A("PF", c, c + 1, 1, p0, p1)
    cP, cG, cGH, cJ, cJ3, cROT, cGHR = pf(0), pf(2), pf(3), pf(4), pf(5), pf(6), pf(7)
    co = lambda c, p0=0, p1=128: A("CO", c, c + 1, 1, p0, p1)
    ID = AF.Identity
    cH, cI, cP8, cR15, cW, cWG, c2GH, c2GHR, cLO, cHI, cJK, cB0, cB1, cTC, cNG, cHS, cTMP, cTM2 = [co(i) for i in range(18)]
    ts(cH, cG, -2.0, AL.mult, cGH, AL.add)
    ts(cI, cG, -16.0, AL.mult, cP, AL.add)
    act(cP8, cP, ID, 8.0)
    act(cR15, cG, ID, 15.0, 16.0)
    ts(cTMP, cH, 14.0, AL.add)
    ts(cW, cG, 16.0, AL.mult, cTMP, AL.add)
    ts(cTM2, cROT, cI, AL.subtract)
    ts(cWG, cTM2, cTMP, AL.add)
    act(c2GH, cGH, ID, 0.0, 2.0)
    act(c2GHR, cGHR, ID, 1.0, 2.0)
    act(cLO, cH, ID, 1.0, -1.0)
    act(cJK, cJ, ID, 0.0, 1024.0)
    act(cB0, cJ, ID, -4128.0 + 8448.0 - 16384.0)
    act(cB1, cJ, ID, -24.0 + 8448.0 - 16384.0)
    act(cNG, cG, ID, 0.0, -16.0)
    cHI = cH
    ts(co(20, 0, 64), pf(0, 0, 64), 2.0, AL.mult, pf(4, 0, 64), AL.subtract)
    ts(co(21, 64, 96), pf(5, 64, 96), -3.0, AL.mult, -256.0, AL.add)
    ts(co(20, 64, 96), pf(0, 64, 96), 4.0, AL.mult, co(21, 64, 96), AL.add)
    ts(co(20, 96, 128), pf(0, 96, 128), 16.0, AL.mult, -1532.0, AL.add)
    ts(cTC, co(20), 8.0, AL.add)
    ts(A("S8"), A("ROW", 0, 8), cJ, AL.is_equal)
    s8 = lambda j: A("S8", j, j + 1)
    ts(co(22), s8(1), 1024.0, AL.mult)
    ts(cHS, co(22), s8(0), AL.subtract)
    act(A("UC"), A("UC"), ID, cH)
    act(A("UW"), A("UV"), ID, cNG)

    M = lambda i: A("MM", 128 * i, 128 * i + 128)
    mI, mNI, mI17, mI8, mI2K, mI16K, mIOFF, mBLK, mH, mHS, mH8, mHN8, mH2, mHN3, mHN0, mA1, mG1, mAN0, mGN0 = [M(i) for i in range(19)]
    MSt = lambda i: A("MS", 144 * i, 144 * i + 144)
    sl = lambda i, o: A("MS", 144 * i + o, 144 * i + o + 128)
    RW = A("ROW", 0, 144)
    R128 = A("ROW", 0, 128)
    mI32, mROT = A("MF", 0, 128), A("MF", 128, 256)
    FSt = lambda i: A("MF", 256 + 144 * i, 256 + 144 * i + 144)
    fsl = lambda i, o, p0=0, p1=128: A("MF", 256 + 144 * i + o, 256 + 144 * i + o + 128, 1, p0, p1)
    EQ, MU = AL.is_equal, AL.mult
    ts(FSt(2), RW, cTC, EQ)
    ts(MSt(0), RW, cW, EQ, s8(0), MU)
    ts(MSt(1), RW, cW, EQ, s8(1), MU)
    ts(MSt(2), RW, cWG, EQ, s8(1), MU)
    ts(MSt(3), RW, cW, EQ, -8192.0, MU)
    ts(MSt(4), RW, cP8, EQ, cLO, MU)
    ts(MSt(5), RW, cP, EQ, cHI, MU)
    act(MSt(6), MSt(4), ID, 0.0, 32.0)
    act(MSt(7), MSt(5), ID, 0.0, 32.0)
    ts(MSt(8), RW, cR15, EQ, 4096.0, MU)
    act(MSt(9), MSt(8), ID, 0.0, 32.0)
    if TK16:
        ksl = lambda i, o: A("MH", 144 * i + o, 144 * i + o + 128)
        cp(A("MH"), A("MS", 144 * 4, 144 * 6))
    else:
        ksl = fsl
        act(FSt(0), MSt(4), ID)
        act(FSt(1), MSt(5), ID)
    ts(mI, R128, cP, EQ)
    ts(mI32, R128, cP, EQ)
    ts(mROT, R128, cROT, EQ)
    for m, w in ((mNI, -1.0), (mI17, 131072.0), (mI8, 8.0), (mI2K, 2048.0), (mI16K, 16384.0), (mIOFF, -8448.0)):
        act(m, mI, ID, 0.0, w)
    mB = lambda j: A("MB", 128 * j, 128 * j + 128)
    ms(A("ONE"), 1.0)
    for j in range(16):
        add("g", "sel", (mB(j), A("ONE"), [[-16, 8], [0, 16]], -j), [mB(j)], [A("ONE")], 170.0 + 1.66 * 128)
    made = {}

    def diff(j, j2):
        if (j, j2) not in made:
            m = A("MD", 128 * len(made), 128 * len(made) + 128)
            made[(j, j2)] = m
            add("g", "neg", (m, mB(j), [[-16, 8], [0, 16]], -j2), [m], [mB(j)], 170.0 + 1.66 * 128)
        return made[(j, j2)]

    ts(mH, A("F8"), cGH, EQ)
    act(mHS, mH, ID, 0.0, cHS)
    ts(mH8, mH, s8(0), MU, 8.0, MU)
    act(mHN8, mH8, ID, 0.0, -1.0)
    act(mHN0, mH8, ID, 0.0, -0.125)
    act(mH2, mH, ID, 0.0, s8(2))
    ts(mHN3, mH, s8(3), MU, -1.0, MU)
    ts(mA1, A("F4"), c2GH, EQ, s8(1), MU)
    ts(mG1, A("F4"), c2GHR, EQ, s8(1), MU)
    ts(co(23), s8(0), -1.0, MU)
    ts(mAN0, A("F4"), c2GH, EQ, co(23), MU)
    ts(mGN0, A("F4"), c2GHR, EQ, co(23), MU)

    ms(A("U"), 0.0)
    ms(A("X", 4096, YB), 0.0)
    ms(A("D0"), 1.0 / 32)
    ms(A("D0", 0, 2048, 16), 1.0)
    ms(A("D1"), 512.0)
    ms(A("D1", 0, 256, 8), -8388608.0)
    if any("scan" in r for rs in REDS for r in rs):
        ms(A("D2"), 1.0)
        ms(A("D2", 0, 1280, 8), 0.0)
    cp(A("INF", p0=0, p1=104), A("INI", p0=0, p1=104))
    ts(A("K"), A("KI"), -256.0, AL.add)
    for j in range(8):
        if j >= XRV:
            act(A("XR", j, 4096, 8), A("XA"), ID)
        else:
            cp(A("XR", j, 4096, 8), A("XA"))
    D = ["pb0", "pb1", "pb2"]
    SC, M0, M1 = "pb3", "pb4", "pb5"
    mm(A(M0, 0, 256), [(fsl(2, 8 - 8 * h, 64, 104), A("INF", h, 512, 2, 64, 104)) for h in range(2)])
    vtr(A("SPT"), A(M0, 0, 256))
    mm(A(M1, 0, 256), [(fsl(2, 8 - 8 * h, 0, 64), A("INF", h, 512, 2, 0, 64)) for h in range(2)])
    cp(A("NL", 0, 256), A(M1, 0, 256))
    act(A("NMF"), A(M1, 0, 256), ID, -2048.0)

    tw = lambda i: A("TW", 32 * i, 32 * i + 32)
    tf = lambda i: A("TF", 32 * i, 32 * i + 32)
    uq = lambda j: A("U", j, 256, 8)
    UT = lambda t, c0=0, st=1: A("UT", 256 * t + c0, 256 * t + 256, st)
    GU = lambda t, c0=0, st=1: A("GU", 256 * t + c0, 256 * t + 256, st)
    lst = lambda t, i: A("LST", 128 * t + 32 * i, 128 * t + 32 * i + 32)

    def turn_back(t):
        ts(uq(0), tw(0), -256.0, AL.add)
        if t < RO - 1:
            ts(tw(1), tw(0), 3, AL.bitwise_and)
            cp(uq(1), tw(1))
        vtr(UT(t), A("U"))
        if t < RO - 1:
            recv(GU(t), "ru%d" % t, [send(t, GU(t), UT(t), "ru%d" % t, 512)])

    cp(tw(0), A("SPT", 4, 256, 8))
    turn_back(0)
    act(A("SPT"), A("SPT"), ID, 17.0 * 131072 - 512)

    def whole(t):
        last = t == RO - 1
        P, Q = UT(t), UT(t + 1)
        mm(A(M0, 0, 32), [(sl(0, 14 - 2 * q), UT(t, q, 8)) for q in range(8)])
        ts(lst(t, 0), A(M0, 0, 32), 256.0, AL.add)
        act(A("AV"), IND(A("K"), lst(t, 0)), ID)
        mm(A(SC, 256, 512), [(sl(4, 8 - 8 * h), A("AV", h, 512, 2)) for h in range(2)])
        ts(A("CL"), A(SC, 256, 512), 256.0, AL.add)
        tt(A("NQ"), A(SC, 256, 512), A("UC"), AL.not_equal)
        for c in range(2):
            tt(A("EX", 2048 * c, 2048 * c + 2048), IND(A("XA"), A("CL", 128 * c, 128 * c + 128)),
               A("XR", 2048 * c, 2048 * c + 2048), EQ)
        hv = lambda n, kk: A(n, 256 * kk, 256 * kk + 256)
        clo = [(sl(4, 8 - 8 * h), A("K", h, 512, 2)) for h in range(2)]
        chi = [(sl(5, 8 - 8 * h), A("K", h, 512, 2)) for h in range(2)]
        if not last:
            mm(hv(M1, 0), clo + [(mHS, P)])
            ts(A("SM"), hv(M1, 0), cJK, EQ)
            own = [(mI8, A("UW"))] + [(sl(1, 14 - 2 * q), UT(t, q, 8)) for q in range(8)]
            mm(A(M1, 256, 288), own)
            mm(A(M1, 320, 352), own + [(sl(3, 14 - 2 * q), A("SM", q, 256, 8)) for q in range(8)])
            mm(A(M1, 288, 320), [(mI8, A("UW"))] + [(sl(2, 14 - 2 * q), GU(t, q, 8)) for q in range(8)])
            ts(lst(t, 1), A(M1, 256, 288), 2048.0, AL.add)
            ts(lst(t, 2), A(M1, 320, 352), 2048.0 + 8192.0, AL.add, 4096.0, AL.min)
            ts(lst(t, 3), A(M1, 288, 320), 2052.0, AL.add)
            mm(hv(M0, 0), [(mA1, P), (mG1, GU(t))])
            mm(hv(M0, 1), clo + [(mAN0, P), (mGN0, GU(t))])
            ts(hv("MK", 0), hv(M0, 0), cJ3, EQ, -1.0, MU)
            tt(hv("TK", 0), hv(M0, 1), hv("MK", 0), MU)
        order = []
        for j in range(8):
            order += [j, 15 - j]
        held = {}
        na = 0
        nall = 16 - MODE[t].count("v")
        for n, j in enumerate(order):
            o = A("AD", 15 - j, 8192, 16)
            md = MODE[t][j]
            inc = INC and t > 0
            if md == "v":
                b = A(D[2] if inc else D[n % 3])
                mm(b, [(mB(j), A("AV"))])
                tt(o, b, A("K"), AL.not_equal)
            else:
                bn = D[na % 2] if inc else D[n % 3]
                na += 1
                b = A(bn)
                shut = not inc or na > nall - 2
                if inc and bn in held:
                    mm(b, [(diff(j, held[bn]), A("AV"))], False, shut)
                else:
                    mm(b, [(mB(j), A("AV")), (mNI, A("K"))], True, shut)
                held[bn] = j
                act(o, b, AF.Abs)
                if j < 8 and md == "m":
                    ts(o, o, 0.0, AL.not_equal)
                elif j < 8:
                    act(o, o, AF.Sign)
        sc = A(SC, 0, 256)
        mm(sc, [(sl(4, 8 - 8 * h), A("AV", h, 512, 2)) for h in range(2)] + [(mI17, A("NQ"))], True, False)
        for j in range(8):
            mm(sc, [(sl(9, 15 - 8 * h - j), A("AD", 16 * h + 15 - j, 8192, 32))
                    for h in range(2)], False, False)
        mm(sc, [(sl(8, 15 - i), A("EX", i, 4096, 16)) for i in range(16)], False, True)
        vtr(A("TS"), sc)
        scan(A("BS"), A("D1"), A("TS"), 0.0, AL.add, AL.max)
        best = A("BS", 7, 256, 8)
        thr = 17.0 * 131072 - 256
        ts(tf(0), best, 256.0, AL.add)
        tt(tw(2), tf(0), A("SPT", t, 256, 8), AL.max)
        ts(tw(0), tw(2), 511, AL.bitwise_and)
        if not last:
            ts(tf(3), best, thr, AL.is_lt, 16.0, MU)
            ts(tw(4), tw(2), 9, AL.arith_shift_right, 7, AL.bitwise_and)
            ts(uq(3), tw(4), -1.0, MU, 7.0, AL.add)
            ts(tw(5), tw(2), 7, AL.bitwise_and)
            tt(uq(2), tw(5), tf(3), AL.add)
        turn_back(t + 1)
        for c in range(4):
            scan(A("SCN", 2048 * c, 2048 * c + 2048), A("D0"), A("AD", 2048 * c, 2048 * c + 2048), 1.0, AL.add, AL.min)
        rel = lambda kk: [(sl(6 + kk, 8 - 8 * h), A("SCN", 16 * h + 15, 8192, 32)) for h in range(2)]
        for kk in range(2):
            mm(hv(D[0], kk), rel(kk))
        act(A("NF"), A(D[0]), AF.Relu, -1.0, 0.0625)
        act(A("SG"), A(D[0]), AF.Sign, -7.5)
        for kk in range(2):
            mm(hv(D[1], kk), [(mI8, A("UC")), (mHN8, P), (mI16K, hv("NF", kk))])
        for kk in range(2):
            act(hv("TI", kk), hv(D[1], kk), AF.Relu, cB1 if kk else cB0)
        for kk in range(2):
            mm(hv(D[2], kk), rel(kk) + [(mH8, P), (mI2K, hv("SG", kk)), (mIOFF, hv("NF", kk)), (mI32, hv("TI", kk))])
        ts(A("IDX", 512 * t, 512 * t + 512), A(D[2]), 4096.0, AL.add)
        if last:
            for h in range(2):
                mm(hv(M1, h), [(mB(8 * h), Q)])
            for h in range(2):
                act(A("YP", h, 512, 2), hv(M1, h), ID, 256.0)
            dma("s", HB("yp", 0, 8, 0, 512), A("YP", 0, 512, 1, 0, 128, 16), 2048)
            return
        mm(hv(M1, 0), [(mH2, Q)])
        mm(hv(M1, 1), chi + [(mHN0, Q)])
        ts(hv("MK", 1), hv(M1, 0), cJ, EQ, -1.0, MU)
        tt(hv("TK", 1), hv(M1, 1), hv("MK", 1), MU)
        for h in range(2):
            mm(hv(M0, h), [(mI, A("K", h, 512, 2))] + [(ksl(h, 8 - 8 * kk), hv("TK", kk)) for kk in range(2)])
        for h in range(2):
            act(A("K", h, 512, 2), hv(M0, h), ID)
        mm(hv(SC, 1), [(mI32, A("NMF")), (mHN8, P), (mHN3, Q)])
        tt(A("TN"), hv(SC, 1), hv("MK", 1), MU)
        if NMPE:
            mm(hv(SC, 0), [(mI32, A("NMF")), (mI32, A("TN"))])
            ts(A("NL", 256 * t + 256, 256 * t + 512), hv(SC, 0), 2048.0, AL.add)
            if t < RO - 2:
                act(A("NMF"), hv(SC, 0), ID)
        else:
            tt(A("NMF"), A("NMF"), A("TN"), AL.add)
            ts(A("NL", 256 * t + 256, 256 * t + 512), A("NMF"), 2048.0, AL.add)

    def states(t):
        last = t == RO - 1
        SW = A("X", 0, 4096)
        CH, RED, YV = CHS[t], REDS[t], YVS[t]
        cuts = [0, (256 - YV) // 4 * 2, 256 - YV]
        for c0, c1 in zip(cuts, cuts[1:]):
            act(A("X", YB + 16 * c0, YB + 16 * c1), IND(SW, A("NL", 256 * t + c0, 256 * t + c1)), ID)
        if YV:
            cp(A("X", YB + 16 * (256 - YV), 8200), IND(SW, A("NL", 256 * t + 256 - YV, 256 * t + 256)))
        if not last:
            act(A("H8"), IND(A("X", 0, YB), lst(t, 2)), ID, 0.0, 8.0)
        sends = []
        for n in range(len(CH) - 1):
            c0, c1 = CH[n], CH[n + 1]
            e0, e1, u0, u1 = 16 * c0, 16 * c1, 2 * c0, 2 * c1
            w = u1 - u0
            act(A("G", e0, e1), A("X", e0, e1), AF.Sigmoid)
            act(A("G", 4096 + e0, 4096 + e1), A("X", YB + e0, YB + e1), AF.Sigmoid)
            for kk, pn in enumerate(("P1", "P2")):
                b = 512 * t + 256 * kk
                tt(A(pn, e0, e1), IND(A("X"), A("IDX", b + c0, b + c1)), A("G", 4096 * kk + e0, 4096 * kk + e1), MU)
            ob = "pb%d" % (6 + n % 2)
            o = A(ob, 0, w)
            part = lambda pn: [(mI32, A(pn, e0 + k, e1, 8)) for k in range(8)]
            if RED[n] == "pe":
                mm(o, part("P1"), True, False)
                mm(o, part("P2"), False, True)
            elif RED[n] == "dma":
                dma("g", A("P1", e0, e1), A("P2", e0, e1), 4 * (e1 - e0), True)
                mm(o, part("P1"))
            elif RED[n] == "dscan":
                dma("g", A("P1", e0, e1), A("P2", e0, e1), 4 * (e1 - e0), True)
                scan(A("P2", e0, e1), A("D2", 0, e1 - e0), A("P1", e0, e1), 0.0, MU, AL.add)
                mm(o, [(mI32, A("P2", e0 + 7, e1, 8))])
            else:
                mm(o, part("P1"), True, False)
                scan(A("G", 4096 + e0, 4096 + e1), A("D2", 0, e1 - e0), A("P2", e0, e1), 0.0, MU, AL.add)
                mm(o, [(mI32, A("G", 4096 + e0 + 7, 4096 + e1, 8))], False, True)
            if not last and not ZPE:
                tt(A("Z8", u0, u1), o, A("H8", u0, u1), AL.add)
            act(A("OUT", 512 * t + u0, 512 * t + u1), o, ID)
            if last:
                if n in (1, len(CH) - 2):
                    f = 0 if n == 1 else 2 * CH[2]
                    dma("s", HB("yo", 0, 128, 512 * t + f, 512 * t + u1), A("OUT", 512 * t + f, 512 * t + u1), 4 * (u1 - f))
                continue
            if ZPE:
                ou, hh = A("OUT", 512 * t + u0, 512 * t + u1), A("H8", u0, u1)
                mm(A(ob, 176, 176 + w), [(mROT, hh), (mROT, ou)])
                mm(A(ob, 344, 344 + w), [(mI32, hh), (mI32, ou)])
                act(A("SND", 512 * t + u0, 512 * t + u1), A(ob, 176, 176 + w), AF.Sigmoid, 0.0, 0.25)
                act(A("TA", u0, u1), A(ob, 344, 344 + w), AF.Sigmoid, 0.0, 0.25)
            else:
                mm(A(ob, 256, 256 + w), [(mROT, A("Z8", u0, u1))])
                act(A("SND", 512 * t + u0, 512 * t + u1), A(ob, 256, 256 + w), AF.Sigmoid, 0.0, 0.25)
            for grp in SENDS:
                if grp[-1] == n:
                    f = 512 * t + 2 * CH[grp[0]]
                    sends.append(send(t, A("LT", f, 512 * t + u1), A("SND", f, 512 * t + u1), "rt%d" % t, 4 * (512 * t + u1 - f)))
        if last:
            return
        if not ZPE:
            act(A("TA"), A("Z8"), AF.Sigmoid, 0.0, 0.25)
        dma("s", HB("yo", 0, 128, 512 * t, 512 * t + 512), A("OUT", 512 * t, 512 * t + 512), 2048)
        lt = A("LT", 512 * t, 512 * t + 512)
        recv(lt, "rt%d" % t, sends)
        ts(IND(SW, lst(t, 1)), A("TA"), 2.0, MU, -1.0, AL.add)
        ts(IND(SW, lst(t, 3)), lt, 2.0, MU, -1.0, AL.add)

    for t in range(RO):
        tag[0] = 1 + 2 * t
        whole(t)
        tag[0] = 2 + 2 * t
        states(t)
    return ops


def depend(ops):
    hist = {}
    deps = []
    for i, o in enumerate(ops):
        ds = set(o["x"])
        acc = [(n, m, False) for n, m in o["r"]] + [(n, m, True) for n, m in o["w"]]
        for n, m, w in acc:
            ps = n[:2] == "pb"
            for j, m2, w2 in hist.get(n, ()):
                if j == i:
                    continue
                if ps and (ops[j]["e"] != o["e"] or o["e"] == "p"):
                    ds.add(j)
                elif (w or w2) and (m & m2):
                    ds.add(j)
        for n, m, w in acc:
            h = hist.setdefault(n, [])
            if n[:2] == "pb":
                if o["e"] == "p":
                    h[:] = []
                h.append((i, m, w))
            else:
                if w:
                    h[:] = [(j, m2 & ~m, w2) for j, m2, w2 in h if j == i or (m2 & ~m)]
                h.append((i, m, w))
        deps.append(sorted(ds))
    return deps


def simulate(ops, deps, succ, prio, look):
    n = len(ops)
    left = [len(d) for d in deps]
    rdy = [0.0] * n
    start = [0.0] * n
    free = {e: 0.0 for e in "vapgs"}
    pool = {e: [] for e in "vapgs"}
    order = []

    def done(i, s):
        start[i] = s
        order.append(i)
        o = ops[i]
        for k in succ[i]:
            e2 = ops[k]["e"]
            if o["e"] == "p" and e2 == "p":
                f = s + o["d"]
            else:
                f = s + o["d"] + o["l"] + (60.0 if e2 == o["e"] else 120.0)
            if f > rdy[k]:
                rdy[k] = f
            left[k] -= 1
            if left[k] == 0:
                if e2 is None:
                    done(k, rdy[k])
                else:
                    pool[e2].append(k)

    for i in range(n):
        if left[i] == 0:
            pool[ops[i]["e"]].append(i)
    end = 0.0
    while True:
        be, bt = None, 1e30
        for e, p in pool.items():
            if p:
                s = max(free[e], min(rdy[k] for k in p))
                if s < bt:
                    be, bt = e, s
        if be is None:
            break
        i = max((k for k in pool[be] if rdy[k] <= bt + look), key=lambda k: prio[k])
        s = max(bt, rdy[i])
        pool[be].remove(i)
        free[be] = s + ops[i]["d"]
        end = max(end, s + ops[i]["d"] + ops[i]["l"])
        done(i, s)
    return end, order, start


def replay(ops, deps, order, dur):
    fin = [0.0] * len(ops)
    free = {}
    end = 0.0
    for i in order:
        e = ops[i]["e"]
        s = free.get(e, 0.0) if e else 0.0
        for j in deps[i]:
            e2 = ops[j]["e"]
            f = fin[j]
            if not (e == "p" and e2 == "p"):
                f += ops[j]["l"] + (60.0 if e2 == e else 120.0)
            if f > s:
                s = f
        fin[i] = s + dur[i]
        free[e] = fin[i]
        end = max(end, fin[i] + ops[i]["l"])
    return end


def place(key, pred, nxt, dur, eng, rel):
    n = len(dur)
    left = [len(p) for p in pred]
    st = [0.0] * n
    line = {e: [] for e in "vapgs"}
    el = [i for i in range(n) if left[i] == 0]
    while el:
        i = min(el, key=lambda k: key[k])
        el.remove(i)
        s = rel[i]
        for j, lg in pred[i]:
            f = st[j] + dur[j] + lg
            if f > s:
                s = f
        if eng[i]:
            ln = line[eng[i]]
            d = dur[i]
            p = len(ln)
            while p > 0 and ln[p - 1][1] > s:
                p -= 1
            while p < len(ln) and ln[p][0] < s + d:
                s = max(s, ln[p][1])
                p += 1
            ln.insert(p, (s, s + d))
        st[i] = s
        for k in nxt[i]:
            left[k] -= 1
            if left[k] == 0:
                el.append(k)
    return st


def plan():
    ops = program(*COSTS[0])
    deps = depend(ops)
    n = len(ops)
    succ = [[] for _ in range(n)]
    for i, d in enumerate(deps):
        for j in d:
            succ[j].append(i)
    base = [0.0] * n
    for i in range(n - 1, -1, -1):
        base[i] = ops[i]["d"] + ops[i]["l"] + 100.0 + max([base[k] for k in succ[i]], default=0.0)
    seed = [12345]

    def noise():
        seed[0] = (seed[0] * 1103515245 + 12345) % 2147483648
        return seed[0] / 1073741824.0 - 1.0

    other = [[o["d"] for o in program(*c)] for c in COSTS[1:]]
    dur = [o["d"] for o in ops]
    eng = [o["e"] for o in ops]

    def lag(j, i):
        if eng[i] == "p" and eng[j] == "p":
            return 0.0
        return ops[j]["l"] + (60.0 if eng[i] == eng[j] else 120.0)

    fw = [[(j, lag(j, i)) for j in deps[i]] for i in range(n)]
    bw = [[(i, lag(j, i)) for i in succ[j]] for j in range(n)]
    tail = [o["l"] for o in ops]
    zero = [0.0] * n
    best = None
    cur = [-b for b in base] if SEEDS is None else [float(x) for x in SEEDS]
    curs = 1e30
    for it in range(TRIES):
        pr = list(cur)
        kind = it % 3
        if it and kind == 0:
            tg = int((noise() + 1.0) * 4.5)
            sh = 8000.0 * noise() * noise()
            pr = [b + (sh if o["t"] == tg else 0.0) for b, o in zip(cur, ops)]
        elif it and kind == 1:
            lo = int((noise() + 1.0) * n / 2)
            w = int(5 + 30 * (noise() + 1.0))
            sh = 5000.0 * noise() * noise()
            for k in range(lo, min(n, lo + w)):
                pr[k] += sh
        elif it:
            amp = 1500.0 * (noise() + 1.0)
            pr = [b + amp * noise() for b in cur]
        st = place(pr, fw, succ, dur, eng, zero)
        bk = place([-(st[i] + dur[i]) for i in range(n)], bw, deps, dur, eng, tail)
        st = place([-(bk[i] + dur[i]) for i in range(n)], fw, succ, dur, eng, zero)
        order = sorted(range(n), key=lambda i: (st[i], i))
        sc = [replay(ops, deps, order, d) for d in [dur] + other]
        tot = sc[0] + sum(sc)
        if tot <= curs + 1500.0 * (1.0 - it / TRIES) * (noise() + 1.0) ** 2 / 4:
            cur, curs = list(st), tot
        if best is None or tot < best[3]:
            best = (sc[0], order, st, tot, sc)
    cnt = {e: 0 for e in "vapg"}
    known = {e: {} for e in "vapgs"}
    clock = [None] * n
    mark = [None] * n
    steps = []
    total = {}
    for i in best[1]:
        o = ops[i]
        e = o["e"]
        if e is None:
            mark[i] = (o["s"], -o["a"][0])
            clock[i] = {o["s"]: 1}
            total[o["s"]] = -o["a"][0]
            continue
        kn = known[e]
        need = {}
        for j in sorted(deps[i], key=lambda j: -best[2][j]):
            if e == "p" and ops[j]["e"] == "p":
                continue
            s, v = mark[j]
            if kn.get(s, 0) >= max(v, 1):
                continue
            need[s] = v if v < 0 else max(need.get(s, 0), v)
            for s2, v2 in clock[j].items():
                if kn.get(s2, 0) < v2:
                    kn[s2] = v2
        if o["k"] == "dma":
            mark[i] = (o["s"], 16)
        elif o["k"] == "send":
            total["ls"] = total.get("ls", 0) - 1
            mark[i] = None
        else:
            cnt[e] += 1
            mark[i] = (ESEM[e], cnt[e])
        if mark[i]:
            clock[i] = dict(kn)
            clock[i][mark[i][0]] = mark[i][1]
            total[mark[i][0]] = mark[i][1]
        steps.append((i, sorted(need.items())))
    return ops, steps, total, best


_PLAN = {}


def rank_program(g, core, T, topo):
    rank = T.rank_of(core)
    if rank is None:
        return
    if not _PLAN:
        _PLAN["p"] = plan()
    ops, steps, total, _ = _PLAN["p"]
    cores = T.cores
    qs = {"v": g.vector, "a": g.scalar, "p": g.tensor, "g": g, "s": g.sync}
    peer = [cores[(rank + 1 + t % (NR - 1)) % NR] for t in range(RO - 1)]
    source = [cores[(rank - 1 - t % (NR - 1)) % NR] for t in range(RO - 1)]
    sent = [0]

    def R(a):
        if not isinstance(a, tuple):
            return a
        if a[0] == "ind":
            return R(a[1]).indirect(R(a[2]))
        if a[0] == "hbm":
            return T[a[1]][a[2]:a[3], a[4]:a[5]]
        ps = slice(a[2], a[3], a[4]) if a[4] > 1 else slice(a[2], a[3])
        cs = slice(a[5], a[6], a[7]) if a[7] > 1 else slice(a[5], a[6])
        return T[a[1]][ps, cs]

    def count(s, v):
        if v >= 0:
            return v
        if s == "ls":
            return sent[0]
        return -v * len(topo.engines(source[int(s[2])], core))

    for i, need in steps:
        o = ops[i]
        q = qs[o["e"]]
        for s, v in need:
            q.wait_ge(T.sem[s], count(s, v))
        k, a = o["k"], o["a"]
        if k == "ts":
            if a[5] is None:
                ins = q.tensor_scalar(R(a[0]), R(a[1]), R(a[2]), None, a[4])
            else:
                ins = q.tensor_scalar(R(a[0]), R(a[1]), R(a[2]), R(a[3]), a[4], a[5])
        elif k == "tt":
            ins = q.tensor_tensor(R(a[0]), R(a[1]), R(a[2]), a[3])
        elif k == "cp":
            ins = q.tensor_copy(R(a[0]), R(a[1]))
        elif k == "ms":
            ins = q.memset(R(a[0]), a[1])
        elif k == "scan":
            ins = q.tensor_tensor_scan(R(a[0]), R(a[1]), R(a[2]), a[3], a[4], a[5])
        elif k == "tr":
            ins = q.transpose(R(a[0]), R(a[1]))
        elif k == "act":
            ins = q.activation(R(a[0]), R(a[1]), a[2], bias=R(a[3]), scale=R(a[4]))
        elif k == "mm":
            for n, (l, r) in enumerate(a[1]):
                ins = q.matmul(R(a[0]), R(l), R(r), a[2] and n == 0, a[3] and n == len(a[1]) - 1)
        elif k == "iota":
            if SB[a[0][1]][1] == I32:
                ins = q.iota(R(a[0]), a[1], a[2], a[3])
            else:
                ins = q.iota(R(a[0]), a[1], a[2], a[3], allow_small_or_imprecise_dtypes=True)
        elif k == "sel":
            ins = q.affine_select(R(a[0]), R(a[1]), a[2], AL.is_equal, 0.0, a[3], 1)
        elif k == "neg":
            ins = q.affine_select(R(a[0]), R(a[1]), a[2], AL.not_equal, -1.0, a[3], 1)
        elif k == "dma":
            if a[2]:
                ins = q.dma_start(R(a[0]), R(a[1]), accum_op=AL.add)
            else:
                ins = q.dma_start(R(a[0]), R(a[1]))
            ins.then_inc(T.sem[o["s"]], 16)
            continue
        else:
            dst = peer[a[0]]
            rid, pid, _se = topo.addr(dst)
            q.remote_dma(R(a[1]), R(a[2]), T.sem[a[3]], T.sem.ls, pid, rid, topo.mask(core, dst))
            sent[0] += len(topo.engines(core, dst))
            continue
        ins.then_inc(T.sem[ESEM[o["e"]]], 1)
    for s, v in sorted(total.items()):
        g.wait_ge(T.sem[s], count(s, v))
